import numpy as np
import ml_dtypes


def mxq(x, axis, fmt="e4m3"):
    dtype, down = {"e4m3": (ml_dtypes.float8_e4m3fn, 7), "e5m2": (ml_dtypes.float8_e5m2, 14)}[fmt]
    v = np.moveaxis(np.asarray(x, np.float32).astype(ml_dtypes.bfloat16).astype(np.float64), axis, -1)
    blocks = v.reshape(v.shape[:-1] + (-1, 32))
    amax = np.abs(blocks).max(-1, keepdims=True)
    byte = np.maximum(np.where(amax > 0, np.frexp(amax)[1] - 1 + 127, 0) - down, 1)
    scale = np.exp2(byte - 127.0)
    codes = (blocks / scale).astype(np.float32).astype(dtype).astype(np.float64)
    return np.moveaxis((codes * scale).reshape(v.shape), -1, axis)


WIDE = False


def mx_kscale(k):
    if not WIDE:
        return np.ones(k)
    levels = np.array([10, -10, 5, -5, 0])
    if k % 512:
        return np.exp2(np.random.permutation(np.resize(levels, k // 32))).repeat(32)
    a = np.empty((k // 512, 16))
    for p in range(k // 512):
        a[p, :8] = np.random.permutation(np.resize(levels, 8))
        for g in range(8):
            far = levels[np.abs(levels - a[p, g]) >= 10]
            a[p, g + 8] = far[np.random.randint(len(far))]
    return np.exp2(a.ravel()).repeat(32)


def f64(x):
    return np.asarray(x).astype(np.float64)


def striped(idx):
    return np.tile(idx.reshape(-1, 16).T, (8, 1)).astype(np.uint16)


def unstriped(offs):
    return offs[:16].T.reshape(-1).astype(np.int64)


def pack_weight(w):
    k, n = w.shape
    w = f64(np.asarray(w, np.float32).astype(ml_dtypes.bfloat16)).reshape(k // 32, 32, n)
    amax = np.abs(w).max(1)
    byte = np.clip(np.where(amax > 0, np.frexp(amax)[1] - 1 + 127 - 7, 1), 1, 254)
    scaled = (w * np.exp2(127.0 - byte)[:, None, :]).reshape(k, n).astype(np.float32)
    words = np.ascontiguousarray(scaled.reshape(k // 512, 128, 4, n).transpose(0, 1, 3, 2)).astype(ml_dtypes.float8_e4m3fn).view(np.uint8)
    return words, np.ascontiguousarray(byte.astype(np.uint8).reshape(k // 512, 16, n))


def unpack_weight(words, scales):
    g, p, n, _ = words.shape
    vals = np.ascontiguousarray(words).view(ml_dtypes.float8_e4m3fn).astype(np.float64) * np.repeat(np.exp2(scales.astype(np.float64) - 127.0), 8, axis=1)[..., None]
    return vals.transpose(0, 1, 3, 2).reshape(g * 512, n)


K, T, E, C, N = 512, 512, 8, 128, 128


def by_expert(wq, xq):
    return np.concatenate([wq[e].T @ xq[:, e * C:(e + 1) * C] for e in range(E)], axis=1)


def setup_inputs():
    n = np.random.standard_normal
    s = mx_kscale(K)[:, None]
    first = np.random.permutation(np.repeat(np.arange(E), T // E))
    second = (first + 1 + np.random.permutation(np.repeat(np.arange(E - 1), -(-T // (E - 1)))[:T])) % E
    while np.bincount(second, minlength=E).max() != T // E:
        load = np.bincount(second, minlength=E); hi, lo = int(load.argmax()), int(load.argmin())
        t = np.flatnonzero((second == hi) & (first != lo))[0]; second[t] = lo
    slot_token = np.empty(E * C, np.int64); pos = np.empty((2, T), np.int64); fill = np.zeros(E, np.int64)
    place = np.stack([np.random.permutation(C) for _ in range(E)])
    for r, deal in enumerate((first, second)):
        for t in np.random.permutation(T):
            e = deal[t]; j = e * C + place[e, fill[e]]; fill[e] += 1; slot_token[j] = t; pos[r, t] = j
    g = np.random.uniform(0.2, 0.8, T)
    packed = [pack_weight(m) for m in n((E, K, N)) / np.sqrt(K) / s[None]]
    return {
        "xT": (n((K, T)) * s).astype(np.float32),
        "w_words": np.stack([m[0] for m in packed]),
        "w_scales": np.stack([m[1] for m in packed]),
        "gate": np.stack([np.tile(g, (N, 1)), np.tile(1.0 - g, (N, 1))]).astype(np.float32),
        "offs": striped(slot_token),
        "pos1": striped(pos[0]),
        "pos2": striped(pos[1]),
    }


def reference(xT, w_words, w_scales, gate, offs, pos1, pos2):
    idx = unstriped(offs)
    xq = mxq(f64(xT)[:, idx], 0, "e4m3")
    w = np.stack([unpack_weight(w_words[e], w_scales[e]) for e in range(E)])
    y = by_expert(w, xq)
    return f64(gate[0]) * y[:, unstriped(pos1)] + f64(gate[1]) * y[:, unstriped(pos2)]

@@ -1,0 +1,104 @@
+from contextlib import ExitStack
+
+import concourse.mybir as mybir
+
+F32 = mybir.dt.float32
+BF16 = mybir.dt.bfloat16
+U32 = mybir.dt.uint32
+I32 = mybir.dt.int32
+U16 = mybir.dt.uint16
+U8 = mybir.dt.uint8
+FP8X4 = mybir.dt.float8_e4m3fn_x4
+MULT = mybir.AluOpType.mult
+ADD = mybir.AluOpType.add
+
+K, T, E, C, N = 512, 512, 8, 128, 128
+P = 128
+SLOTS = E * C
+FLOPS = 2 * K * N * SLOTS
+
+CUT = 256
+N_CUTS = SLOTS // CUT
+HALF = 256
+
+
+def tile_routed_moe_kernel(tc, xT, w_words, w_scales, gate, offs, pos1, pos2, out):
+    nc = tc.nc
+    with ExitStack() as ctx:
+        lists = ctx.enter_context(tc.tile_pool(name="lists", bufs=1))
+        held = ctx.enter_context(tc.tile_pool(name="held", bufs=1))
+        psum = ctx.enter_context(tc.psum_pool(name="psum", bufs=4))
+
+        offs_t = lists.tile([P, SLOTS // 16], U16, name="offs_t")
+        nc.sync.dma_start(offs_t[:], offs)
+
+        planes = []
+        x_view = xT.rearrange("(p t) n -> t p n", t=4)
+        for t in range(4):
+            plane = held.tile([P, T], F32, name="plane%d" % t)
+            nc.sync.dma_start(plane[:], x_view[t])
+            planes.append(plane)
+
+        w_codes = held.tile([P, E, N], U32, name="w_codes", align_bytes=64)
+        nc.sync.dma_start(w_codes[:].bitcast(I32), w_words.rearrange("e a p n r -> p (e a) (n r)").bitcast(I32))
+
+        w_plane = held.tile([P, E, N], U8, name="w_plane", align_bytes=64)
+        nc.vector.memset(w_plane[:].rearrange("p e n -> p (e n)").bitcast(I32), 0)
+        s_view = w_scales.rearrange("e a (q r) n -> r q (e a) n", r=4)
+        for r in range(4):
+            nc.sync.dma_start(w_plane[r:P:32, :, :].bitcast(I32), s_view[r].bitcast(I32))
+
+        pos1_t = lists.tile([P, T // 16], U16, name="pos1_t")
+        nc.sync.dma_start(pos1_t[:], pos1)
+        pos2_t = lists.tile([P, T // 16], U16, name="pos2_t")
+        nc.sync.dma_start(pos2_t[:], pos2)
+        gate_t = held.tile([P, 2, T], F32, name="gate_t")
+        nc.sync.dma_start(gate_t[:], gate.rearrange("g n t -> n g t"))
+
+        y = held.tile([P, SLOTS], F32, name="y")
+
+        grouped = {}
+
+        def gather(s):
+            g4 = held.tile([P, 4, CUT], F32, name="g4_%d" % s)
+            cols = offs_t[:, s * (CUT // 16):(s + 1) * (CUT // 16)]
+            for t in range(4):
+                nc.vector.tensor_copy(g4[:, t, :], planes[t][:].indirect(cols))
+            gr = held.tile([P, CUT, 4], BF16, name="grouped%d" % s, align_bytes=64)
+            nc.scalar.copy(gr[:], g4[:].rearrange("p t c -> p c t"))
+            grouped[s] = gr
+
+        def multiply(s):
+            codes = held.tile([P, CUT], U32, name="codes%d" % s, align_bytes=64)
+            plane = held.tile([P, CUT], U8, name="xplane%d" % s, align_bytes=64)
+            nc.vector.quantize_mx(out=codes[:].bitcast(FP8X4), scales=plane[:], in_=grouped[s][:].rearrange("p c t -> p (c t)"))
+            acc = psum.tile([P, CUT], F32, name="acc")
+            for j in range(CUT // C):
+                e = s * (CUT // C) + j
+                nc.tensor.matmul_mx(
+                    out=acc[:, j * C:(j + 1) * C],
+                    lhsT=w_codes[:, e, :].bitcast(FP8X4),
+                    lhsT_scale=w_plane[:, e, :],
+                    rhs=codes[:, j * C:(j + 1) * C].bitcast(FP8X4),
+                    rhs_scale=plane[:, j * C:(j + 1) * C],
+                    start=True,
+                    stop=True,
+                )
+            nc.scalar.copy(y[:, s * CUT:(s + 1) * CUT], acc[:])
+
+        gather(0)
+        for s in range(1, N_CUTS):
+            gather(s)
+            multiply(s - 1)
+        multiply(N_CUTS - 1)
+
+        for h in range(T // HALF):
+            tok = slice(h * HALF, (h + 1) * HALF)
+            cols = slice(h * (HALF // 16), (h + 1) * (HALF // 16))
+            first = held.tile([P, HALF], F32, name="first%d" % h)
+            second = held.tile([P, HALF], F32, name="second%d" % h)
+            total = held.tile([P, HALF], F32, name="total%d" % h)
+            nc.vector.tensor_tensor(first[:], y[:].indirect(pos1_t[:, cols]), gate_t[:, 0, tok], MULT)
+            nc.vector.tensor_tensor(second[:], y[:].indirect(pos2_t[:, cols]), gate_t[:, 1, tok], MULT)
+            nc.vector.tensor_tensor(total[:], first[:], second[:], ADD)
+            nc.sync.dma_start(out[:, tok], total[:])

@@ -11,15 +11,21 @@ U8 = mybir.dt.uint8
 FP8X4 = mybir.dt.float8_e4m3fn_x4
 MULT = mybir.AluOpType.mult
 ADD = mybir.AluOpType.add
+COPY = mybir.ActivationFunctionType.Copy
 
 K, T, E, C, N = 512, 512, 8, 128, 128
 P = 128
 SLOTS = E * C
 FLOPS = 2 * K * N * SLOTS
 
-CUT = 256
-N_CUTS = SLOTS // CUT
-HALF = 256
+V_CUTS = [256,256,256,128]
+F_EXPERTS = 1
+CAST = "scalar"
+PIECES = [256,256]
+LAG = 1
+F_AFTER = 1
+LAST_IL = "scalar"
+IL = "scalar"
 
 
 def tile_routed_moe_kernel(tc, xT, w_words, w_scales, gate, offs, pos1, pos2, out):
@@ -27,7 +33,8 @@ def tile_routed_moe_kernel(tc, xT, w_words, w_scales, gate, offs, pos1, pos2, ou
     with ExitStack() as ctx:
         lists = ctx.enter_context(tc.tile_pool(name="lists", bufs=1))
         held = ctx.enter_context(tc.tile_pool(name="held", bufs=1))
-        psum = ctx.enter_context(tc.psum_pool(name="psum", bufs=4))
+        psum = ctx.enter_context(tc.psum_pool(name="psum", bufs=6))
+        ring = ctx.enter_context(tc.tile_pool(name="ring", bufs=2))
 
         offs_t = lists.tile([P, SLOTS // 16], U16, name="offs_t")
         nc.sync.dma_start(offs_t[:], offs)
@@ -57,24 +64,13 @@ def tile_routed_moe_kernel(tc, xT, w_words, w_scales, gate, offs, pos1, pos2, ou
 
         y = held.tile([P, SLOTS], F32, name="y")
 
-        grouped = {}
-
-        def gather(s):
-            g4 = held.tile([P, 4, CUT], F32, name="g4_%d" % s)
-            cols = offs_t[:, s * (CUT // 16):(s + 1) * (CUT // 16)]
-            for t in range(4):
-                nc.vector.tensor_copy(g4[:, t, :], planes[t][:].indirect(cols))
-            gr = held.tile([P, CUT, 4], BF16, name="grouped%d" % s, align_bytes=64)
-            nc.scalar.copy(gr[:], g4[:].rearrange("p t c -> p c t"))
-            grouped[s] = gr
-
-        def multiply(s):
-            codes = held.tile([P, CUT], U32, name="codes%d" % s, align_bytes=64)
-            plane = held.tile([P, CUT], U8, name="xplane%d" % s, align_bytes=64)
-            nc.vector.quantize_mx(out=codes[:].bitcast(FP8X4), scales=plane[:], in_=grouped[s][:].rearrange("p c t -> p (c t)"))
-            acc = psum.tile([P, CUT], F32, name="acc")
-            for j in range(CUT // C):
-                e = s * (CUT // C) + j
+        def multiply(slot0, n, gr):
+            codes = held.tile([P, n], U32, name="codes%d" % slot0, align_bytes=64)
+            plane = held.tile([P, n], U8, name="xplane%d" % slot0, align_bytes=64)
+            nc.vector.quantize_mx(out=codes[:].bitcast(FP8X4), scales=plane[:], in_=gr[:].rearrange("p c t -> p (c t)"))
+            acc = psum.tile([P, 256], F32, name="acc")
+            for j in range(n // C):
+                e = slot0 // C + j
                 nc.tensor.matmul_mx(
                     out=acc[:, j * C:(j + 1) * C],
                     lhsT=w_codes[:, e, :].bitcast(FP8X4),
@@ -84,21 +80,61 @@ def tile_routed_moe_kernel(tc, xT, w_words, w_scales, gate, offs, pos1, pos2, ou
                     start=True,
                     stop=True,
                 )
-            nc.scalar.copy(y[:, s * CUT:(s + 1) * CUT], acc[:])
+            nc.scalar.copy(y[:, slot0:slot0 + n], acc[:, 0:n])
 
-        gather(0)
-        for s in range(1, N_CUTS):
-            gather(s)
-            multiply(s - 1)
-        multiply(N_CUTS - 1)
+        f_group = None
+        if F_EXPERTS:
+            xb = held.tile([P, 4, T], BF16, name="xb")
+            for t in range(4):
+                if CAST == "scalar":
+                    nc.scalar.copy(xb[:, t, :], planes[t][:])
+                elif CAST == "gpsimd":
+                    nc.gpsimd.tensor_scalar(xb[:, t, :], planes[t][:], 1.0, 0.0, MULT, ADD)
+                else:
+                    nc.vector.tensor_copy(xb[:, t, :], planes[t][:])
+            f0 = SLOTS - F_EXPERTS * C
+            gf = held.tile([P, F_EXPERTS * C, 4], BF16, name="grouped_f", align_bytes=64)
+            for j in range(F_EXPERTS):
+                e = E - F_EXPERTS + j
+                for t in range(4):
+                    nc.scalar.activation(gf[:, j * C:(j + 1) * C, t], xb[:, t, :].indirect(offs_t[:, e * (C // 16):(e + 1) * (C // 16)]), COPY)
+            f_group = (f0, F_EXPERTS * C, gf)
 
-        for h in range(T // HALF):
-            tok = slice(h * HALF, (h + 1) * HALF)
-            cols = slice(h * (HALF // 16), (h + 1) * (HALF // 16))
-            first = held.tile([P, HALF], F32, name="first%d" % h)
-            second = held.tile([P, HALF], F32, name="second%d" % h)
-            total = held.tile([P, HALF], F32, name="total%d" % h)
+        done = []
+        slot0 = 0
+        for i, n in enumerate(V_CUTS):
+            g4 = ring.tile([P, 4, n], F32, name="g4")
+            cols = offs_t[:, slot0 // 16:(slot0 + n) // 16]
+            if i in [1]:
+                nc.vector.tensor_copy(g4[:, :, 0:1], planes[3][:, 0:4].rearrange("p (t o) -> p t o", o=1))
+            for t in range(4):
+                nc.vector.tensor_copy(g4[:, t, :], planes[t][:].indirect(cols))
+            gr = held.tile([P, n, 4], BF16, name="grouped%d" % i, align_bytes=64)
+            src = g4[:].rearrange("p t c -> p c t")
+            if i == len(V_CUTS) - 1 and LAST_IL == "vector":
+                nc.vector.tensor_copy(gr[:], src)
+            elif IL == "gpsimd":
+                nc.gpsimd.tensor_scalar(gr[:], src, 1.0, 0.0, MULT, ADD)
+            else:
+                nc.scalar.copy(gr[:], src)
+            done.append((slot0, n, gr))
+            slot0 += n
+            if f_group is not None and i == F_AFTER:
+                multiply(*f_group)
+            if i >= LAG:
+                multiply(*done[i - LAG])
+        for i in range(len(V_CUTS) - LAG, len(V_CUTS)):
+            multiply(*done[i])
+
+        t0 = 0
+        for h, n in enumerate(PIECES):
+            tok = slice(t0, t0 + n)
+            cols = slice(t0 // 16, (t0 + n) // 16)
+            first = held.tile([P, n], F32, name="first%d" % h)
+            second = held.tile([P, n], F32, name="second%d" % h)
+            total = held.tile([P, n], F32, name="total%d" % h)
             nc.vector.tensor_tensor(first[:], y[:].indirect(pos1_t[:, cols]), gate_t[:, 0, tok], MULT)
             nc.vector.tensor_tensor(second[:], y[:].indirect(pos2_t[:, cols]), gate_t[:, 1, tok], MULT)
             nc.vector.tensor_tensor(total[:], first[:], second[:], ADD)
             nc.sync.dma_start(out[:, tok], total[:])
+            t0 += n

@@ -18,14 +18,11 @@ P = 128
 SLOTS = E * C
 FLOPS = 2 * K * N * SLOTS
 
-V_CUTS = [256,256,256,128]
-F_EXPERTS = 1
-CAST = "scalar"
+CUTS = [[0,256],[256,256],[512,128]]
+STEPS = ["cast","g0","il0:g","f5","g1","il1:g","f6","g2","il2:g","f7","m0:s","mf5:s","mf6:s","m1:v","m2:v","mf7:v"]
+TOUCH = [1,2]
+RING = 3
 PIECES = [256,256]
-LAG = 1
-F_AFTER = 1
-LAST_IL = "scalar"
-IL = "scalar"
 
 
 def tile_routed_moe_kernel(tc, xT, w_words, w_scales, gate, offs, pos1, pos2, out):
@@ -33,8 +30,8 @@ def tile_routed_moe_kernel(tc, xT, w_words, w_scales, gate, offs, pos1, pos2, ou
     with ExitStack() as ctx:
         lists = ctx.enter_context(tc.tile_pool(name="lists", bufs=1))
         held = ctx.enter_context(tc.tile_pool(name="held", bufs=1))
-        psum = ctx.enter_context(tc.psum_pool(name="psum", bufs=6))
-        ring = ctx.enter_context(tc.tile_pool(name="ring", bufs=2))
+        psum = ctx.enter_context(tc.psum_pool(name="psum", bufs=8))
+        ring = ctx.enter_context(tc.tile_pool(name="ring", bufs=RING))
 
         offs_t = lists.tile([P, SLOTS // 16], U16, name="offs_t")
         nc.sync.dma_start(offs_t[:], offs)
@@ -63,8 +60,11 @@ def tile_routed_moe_kernel(tc, xT, w_words, w_scales, gate, offs, pos1, pos2, ou
         nc.sync.dma_start(gate_t[:], gate.rearrange("g n t -> n g t"))
 
         y = held.tile([P, SLOTS], F32, name="y")
+        xb = held.tile([P, 4, T], BF16, name="xb")
+        g4s = {}
+        groups = {}
 
-        def multiply(slot0, n, gr):
+        def multiply(slot0, n, gr, eng):
             codes = held.tile([P, n], U32, name="codes%d" % slot0, align_bytes=64)
             plane = held.tile([P, n], U8, name="xplane%d" % slot0, align_bytes=64)
             nc.vector.quantize_mx(out=codes[:].bitcast(FP8X4), scales=plane[:], in_=gr[:].rearrange("p c t -> p (c t)"))
@@ -80,51 +80,50 @@ def tile_routed_moe_kernel(tc, xT, w_words, w_scales, gate, offs, pos1, pos2, ou
                     start=True,
                     stop=True,
                 )
-            nc.scalar.copy(y[:, slot0:slot0 + n], acc[:, 0:n])
-
-        f_group = None
-        if F_EXPERTS:
-            xb = held.tile([P, 4, T], BF16, name="xb")
-            for t in range(4):
-                if CAST == "scalar":
-                    nc.scalar.copy(xb[:, t, :], planes[t][:])
-                elif CAST == "gpsimd":
-                    nc.gpsimd.tensor_scalar(xb[:, t, :], planes[t][:], 1.0, 0.0, MULT, ADD)
-                else:
-                    nc.vector.tensor_copy(xb[:, t, :], planes[t][:])
-            f0 = SLOTS - F_EXPERTS * C
-            gf = held.tile([P, F_EXPERTS * C, 4], BF16, name="grouped_f", align_bytes=64)
-            for j in range(F_EXPERTS):
-                e = E - F_EXPERTS + j
-                for t in range(4):
-                    nc.scalar.activation(gf[:, j * C:(j + 1) * C, t], xb[:, t, :].indirect(offs_t[:, e * (C // 16):(e + 1) * (C // 16)]), COPY)
-            f_group = (f0, F_EXPERTS * C, gf)
-
-        done = []
-        slot0 = 0
-        for i, n in enumerate(V_CUTS):
-            g4 = ring.tile([P, 4, n], F32, name="g4")
-            cols = offs_t[:, slot0 // 16:(slot0 + n) // 16]
-            if i in [1]:
-                nc.vector.tensor_copy(g4[:, :, 0:1], planes[3][:, 0:4].rearrange("p (t o) -> p t o", o=1))
-            for t in range(4):
-                nc.vector.tensor_copy(g4[:, t, :], planes[t][:].indirect(cols))
-            gr = held.tile([P, n, 4], BF16, name="grouped%d" % i, align_bytes=64)
-            src = g4[:].rearrange("p t c -> p c t")
-            if i == len(V_CUTS) - 1 and LAST_IL == "vector":
-                nc.vector.tensor_copy(gr[:], src)
-            elif IL == "gpsimd":
-                nc.gpsimd.tensor_scalar(gr[:], src, 1.0, 0.0, MULT, ADD)
+            if eng == "v":
+                nc.vector.tensor_copy(y[:, slot0:slot0 + n], acc[:, 0:n])
             else:
-                nc.scalar.copy(gr[:], src)
-            done.append((slot0, n, gr))
-            slot0 += n
-            if f_group is not None and i == F_AFTER:
-                multiply(*f_group)
-            if i >= LAG:
-                multiply(*done[i - LAG])
-        for i in range(len(V_CUTS) - LAG, len(V_CUTS)):
-            multiply(*done[i])
+                nc.scalar.copy(y[:, slot0:slot0 + n], acc[:, 0:n])
+
+        for step in STEPS:
+            parts = step.split(":")
+            op = parts[0]
+            eng = parts[1] if len(parts) > 1 else "s"
+            if op == "cast":
+                for t in range(4):
+                    nc.scalar.copy(xb[:, t, :], planes[t][:])
+            elif op.startswith("mf"):
+                multiply(*groups[op[1:]], eng)
+            elif op.startswith("f"):
+                e = int(op[1:])
+                gf = held.tile([P, C, 4], BF16, name="grouped_f%d" % e, align_bytes=64)
+                for t in range(4):
+                    nc.scalar.activation(gf[:, :, t], xb[:, t, :].indirect(offs_t[:, e * (C // 16):(e + 1) * (C // 16)]), COPY)
+                groups[op] = (e * C, C, gf)
+            elif op.startswith("g"):
+                i = int(op[1:])
+                slot0, n = CUTS[i]
+                g4 = ring.tile([P, 4, n], F32, name="g4")
+                if i in TOUCH:
+                    nc.vector.tensor_copy(g4[:, :, 0:1], planes[3][:, 0:4].rearrange("p (t o) -> p t o", o=1))
+                cols = offs_t[:, slot0 // 16:(slot0 + n) // 16]
+                for t in range(4):
+                    nc.vector.tensor_copy(g4[:, t, :], planes[t][:].indirect(cols))
+                g4s[i] = g4
+            elif op.startswith("il"):
+                i = int(op[2:])
+                slot0, n = CUTS[i]
+                gr = held.tile([P, n, 4], BF16, name="grouped%d" % i, align_bytes=64)
+                src = g4s[i][:].rearrange("p t c -> p c t")
+                if eng == "v":
+                    nc.vector.tensor_copy(gr[:], src)
+                elif eng == "g":
+                    nc.gpsimd.tensor_scalar(gr[:], src, 1.0, 0.0, MULT, ADD)
+                else:
+                    nc.scalar.copy(gr[:], src)
+                groups[str(i)] = (slot0, n, gr)
+            elif op.startswith("m"):
+                multiply(*groups[op[1:]], eng)
 
         t0 = 0
         for h, n in enumerate(PIECES):

@@ -19,7 +19,7 @@ SLOTS = E * C
 FLOPS = 2 * K * N * SLOTS
 
 CUTS = [[0,256],[256,256],[512,128]]
-STEPS = ["cast","g0","il0:g","f5","g1","il1:g","f6","g2","il2:g","f7","m0:s","mf5:s","mf6:s","m1:v","m2:v","mf7:v"]
+STEPS = ["cast:s:0","touch:s","cast:g:1,2,3","f:5,6","g0","il0:g","g1","il1:g","f:7","g2","m0:s","il2:v","mf5:s","m1:s","mf6:v","m2:v","mf7:v"]
 TOUCH = [1,2]
 RING = 3
 PIECES = [256,256]
@@ -32,6 +32,7 @@ def tile_routed_moe_kernel(tc, xT, w_words, w_scales, gate, offs, pos1, pos2, ou
         held = ctx.enter_context(tc.tile_pool(name="held", bufs=1))
         psum = ctx.enter_context(tc.psum_pool(name="psum", bufs=8))
         ring = ctx.enter_context(tc.tile_pool(name="ring", bufs=RING))
+        qring = ctx.enter_context(tc.tile_pool(name="qring", bufs=3))
 
         offs_t = lists.tile([P, SLOTS // 16], U16, name="offs_t")
         nc.sync.dma_start(offs_t[:], offs)
@@ -63,10 +64,12 @@ def tile_routed_moe_kernel(tc, xT, w_words, w_scales, gate, offs, pos1, pos2, ou
         xb = held.tile([P, 4, T], BF16, name="xb")
         g4s = {}
         groups = {}
+        for i, cut in enumerate(CUTS):
+            g4s[i] = held.tile([P, 4, cut[1]], F32, name="g4_%d" % i)
 
         def multiply(slot0, n, gr, eng):
-            codes = held.tile([P, n], U32, name="codes%d" % slot0, align_bytes=64)
-            plane = held.tile([P, n], U8, name="xplane%d" % slot0, align_bytes=64)
+            codes = qring.tile([P, n], U32, name="codes", align_bytes=64)
+            plane = qring.tile([P, n], U8, name="xplane", align_bytes=64)
             nc.vector.quantize_mx(out=codes[:].bitcast(FP8X4), scales=plane[:], in_=gr[:].rearrange("p c t -> p (c t)"))
             acc = psum.tile([P, 256], F32, name="acc")
             for j in range(n // C):
@@ -89,9 +92,27 @@ def tile_routed_moe_kernel(tc, xT, w_words, w_scales, gate, offs, pos1, pos2, ou
             parts = step.split(":")
             op = parts[0]
             eng = parts[1] if len(parts) > 1 else "s"
-            if op == "cast":
+            if op == "touch":
+                for i in TOUCH:
+                    src = planes[3][:, 0:4].rearrange("p (t o) -> p t o", o=1)
+                    if eng == "v":
+                        nc.vector.tensor_copy(g4s[i][:, :, 0:1], src)
+                    else:
+                        nc.scalar.copy(g4s[i][:, :, 0:1], src)
+            elif op == "cast":
+                for t in [int(v) for v in parts[2].split(",")]:
+                    if eng == "g":
+                        nc.gpsimd.tensor_scalar(xb[:, t, :], planes[t][:], 1.0, 0.0, MULT, ADD)
+                    else:
+                        nc.scalar.copy(xb[:, t, :], planes[t][:])
+            elif op == "f":
+                experts = [int(v) for v in eng.split(",")]
+                for e in experts:
+                    gf = held.tile([P, C, 4], BF16, name="grouped_f%d" % e, align_bytes=64)
+                    groups["f%d" % e] = (e * C, C, gf)
                 for t in range(4):
-                    nc.scalar.copy(xb[:, t, :], planes[t][:])
+                    for e in experts:
+                        nc.scalar.activation(groups["f%d" % e][2][:, :, t], xb[:, t, :].indirect(offs_t[:, e * (C // 16):(e + 1) * (C // 16)]), COPY)
             elif op.startswith("mf"):
                 multiply(*groups[op[1:]], eng)
             elif op.startswith("f"):
@@ -103,13 +124,10 @@ def tile_routed_moe_kernel(tc, xT, w_words, w_scales, gate, offs, pos1, pos2, ou
             elif op.startswith("g"):
                 i = int(op[1:])
                 slot0, n = CUTS[i]
-                g4 = ring.tile([P, 4, n], F32, name="g4")
-                if i in TOUCH:
-                    nc.vector.tensor_copy(g4[:, :, 0:1], planes[3][:, 0:4].rearrange("p (t o) -> p t o", o=1))
+                g4 = g4s[i]
                 cols = offs_t[:, slot0 // 16:(slot0 + n) // 16]
                 for t in range(4):
                     nc.vector.tensor_copy(g4[:, t, :], planes[t][:].indirect(cols))
-                g4s[i] = g4
             elif op.startswith("il"):
                 i = int(op[2:])
                 slot0, n = CUTS[i]

@@ -13,16 +13,20 @@ MULT = mybir.AluOpType.mult
 ADD = mybir.AluOpType.add
 COPY = mybir.ActivationFunctionType.Copy
 
-K, T, E, C, N = 512, 512, 8, 128, 128
 P = 128
-SLOTS = E * C
-FLOPS = 2 * K * N * SLOTS
+PACK = 4
+K, TOKENS, EXPERTS, CAPACITY, FEATURES = 512, 512, 8, 128, 128
+SLOTS = EXPERTS * CAPACITY
+PER_COLUMN = 16
+FLOPS = 2 * K * FEATURES * SLOTS
 
-CUTS = [[0,256],[256,256],[512,128]]
-STEPS = ["cast:s:0","touch:s","cast:g:1,2,3","f:5,6","g0","il0:g","g1","il1:g","f:7","g2","m0:s","il2:v","mf5:s","m1:s","mf6:v","m2:v","mf7:v"]
-TOUCH = [1,2]
-RING = 3
-PIECES = [256,256]
+VECTOR_GROUPS = ((0, 256), (256, 256), (512, 128))
+SCALAR_GROUPS = ((640, 256), (896, 128))
+COMBINE_TOKENS = 256
+
+
+def list_columns(first, count):
+    return slice(first // PER_COLUMN, (first + count) // PER_COLUMN)
 
 
 def tile_routed_moe_kernel(tc, xT, w_words, w_scales, gate, offs, pos1, pos2, out):
@@ -30,128 +34,104 @@ def tile_routed_moe_kernel(tc, xT, w_words, w_scales, gate, offs, pos1, pos2, ou
     with ExitStack() as ctx:
         lists = ctx.enter_context(tc.tile_pool(name="lists", bufs=1))
         held = ctx.enter_context(tc.tile_pool(name="held", bufs=1))
-        psum = ctx.enter_context(tc.psum_pool(name="psum", bufs=8))
-        ring = ctx.enter_context(tc.tile_pool(name="ring", bufs=RING))
-        qring = ctx.enter_context(tc.tile_pool(name="qring", bufs=3))
+        operands = ctx.enter_context(tc.tile_pool(name="operands", bufs=3))
+        psum = ctx.enter_context(tc.psum_pool(name="psum", bufs=len(VECTOR_GROUPS) + len(SCALAR_GROUPS)))
 
-        offs_t = lists.tile([P, SLOTS // 16], U16, name="offs_t")
+        offs_t = lists.tile([P, SLOTS // PER_COLUMN], U16, name="offs_t")
         nc.sync.dma_start(offs_t[:], offs)
 
         planes = []
-        x_view = xT.rearrange("(p t) n -> t p n", t=4)
-        for t in range(4):
-            plane = held.tile([P, T], F32, name="plane%d" % t)
-            nc.sync.dma_start(plane[:], x_view[t])
+        x_planes = xT.rearrange("(p t) n -> t p n", t=PACK)
+        for t in range(PACK):
+            plane = held.tile([P, TOKENS], F32, name="plane%d" % t)
+            nc.sync.dma_start(plane[:], x_planes[t])
             planes.append(plane)
 
-        w_codes = held.tile([P, E, N], U32, name="w_codes", align_bytes=64)
+        w_codes = held.tile([P, EXPERTS, FEATURES], U32, name="w_codes", align_bytes=64)
         nc.sync.dma_start(w_codes[:].bitcast(I32), w_words.rearrange("e a p n r -> p (e a) (n r)").bitcast(I32))
 
-        w_plane = held.tile([P, E, N], U8, name="w_plane", align_bytes=64)
-        nc.vector.memset(w_plane[:].rearrange("p e n -> p (e n)").bitcast(I32), 0)
-        s_view = w_scales.rearrange("e a (q r) n -> r q (e a) n", r=4)
+        w_scale = held.tile([P, EXPERTS, FEATURES], U8, name="w_scale", align_bytes=64)
+        nc.vector.memset(w_scale[:].rearrange("p e n -> p (e n)").bitcast(I32), 0)
+        scale_rows = w_scales.rearrange("e a (q r) n -> r q (e a) n", r=4)
         for r in range(4):
-            nc.sync.dma_start(w_plane[r:P:32, :, :].bitcast(I32), s_view[r].bitcast(I32))
+            nc.sync.dma_start(w_scale[r:P:32, :, :].bitcast(I32), scale_rows[r].bitcast(I32))
 
-        pos1_t = lists.tile([P, T // 16], U16, name="pos1_t")
+        pos1_t = lists.tile([P, TOKENS // PER_COLUMN], U16, name="pos1_t")
         nc.sync.dma_start(pos1_t[:], pos1)
-        pos2_t = lists.tile([P, T // 16], U16, name="pos2_t")
+        pos2_t = lists.tile([P, TOKENS // PER_COLUMN], U16, name="pos2_t")
         nc.sync.dma_start(pos2_t[:], pos2)
-        gate_t = held.tile([P, 2, T], F32, name="gate_t")
+        gate_t = held.tile([P, 2, TOKENS], F32, name="gate_t")
         nc.sync.dma_start(gate_t[:], gate.rearrange("g n t -> n g t"))
 
         y = held.tile([P, SLOTS], F32, name="y")
-        xb = held.tile([P, 4, T], BF16, name="xb")
-        g4s = {}
-        groups = {}
-        for i, cut in enumerate(CUTS):
-            g4s[i] = held.tile([P, 4, cut[1]], F32, name="g4_%d" % i)
+        planes_bf = held.tile([P, PACK, TOKENS], BF16, name="planes_bf")
+        gathered = [held.tile([P, PACK, count], F32, name="gathered%d" % first) for first, count in VECTOR_GROUPS]
+        grouped = {}
+        for first, count in VECTOR_GROUPS + SCALAR_GROUPS:
+            grouped[first] = held.tile([P, count, PACK], BF16, name="grouped%d" % first, align_bytes=64)
 
-        def multiply(slot0, n, gr, eng):
-            codes = qring.tile([P, n], U32, name="codes", align_bytes=64)
-            plane = qring.tile([P, n], U8, name="xplane", align_bytes=64)
-            nc.vector.quantize_mx(out=codes[:].bitcast(FP8X4), scales=plane[:], in_=gr[:].rearrange("p c t -> p (c t)"))
-            acc = psum.tile([P, 256], F32, name="acc")
-            for j in range(n // C):
-                e = slot0 // C + j
+        def gather_on_vector(i):
+            first, count = VECTOR_GROUPS[i]
+            for t in range(PACK):
+                nc.vector.tensor_copy(gathered[i][:, t, :], planes[t][:].indirect(offs_t[:, list_columns(first, count)]))
+
+        def interleaved(i):
+            return gathered[i][:].rearrange("p t c -> p c t")
+
+        def gather_on_scalar(first, count):
+            for t in range(PACK):
+                for c in range(0, count, CAPACITY):
+                    nc.scalar.activation(
+                        grouped[first][:, c:c + CAPACITY, t],
+                        planes_bf[:, t, :].indirect(offs_t[:, list_columns(first + c, CAPACITY)]),
+                        COPY,
+                    )
+
+        def multiply(first, count, copy_out):
+            codes = operands.tile([P, count], U32, name="codes", align_bytes=64)
+            scale = operands.tile([P, count], U8, name="scale", align_bytes=64)
+            nc.vector.quantize_mx(out=codes[:].bitcast(FP8X4), scales=scale[:], in_=grouped[first][:].rearrange("p c t -> p (c t)"))
+            sums = psum.tile([P, count], F32, name="sums")
+            for c in range(0, count, CAPACITY):
+                e = (first + c) // CAPACITY
                 nc.tensor.matmul_mx(
-                    out=acc[:, j * C:(j + 1) * C],
+                    out=sums[:, c:c + CAPACITY],
                     lhsT=w_codes[:, e, :].bitcast(FP8X4),
-                    lhsT_scale=w_plane[:, e, :],
-                    rhs=codes[:, j * C:(j + 1) * C].bitcast(FP8X4),
-                    rhs_scale=plane[:, j * C:(j + 1) * C],
+                    lhsT_scale=w_scale[:, e, :],
+                    rhs=codes[:, c:c + CAPACITY].bitcast(FP8X4),
+                    rhs_scale=scale[:, c:c + CAPACITY],
                     start=True,
                     stop=True,
                 )
-            if eng == "v":
-                nc.vector.tensor_copy(y[:, slot0:slot0 + n], acc[:, 0:n])
-            else:
-                nc.scalar.copy(y[:, slot0:slot0 + n], acc[:, 0:n])
+            copy_out(y[:, first:first + count], sums[:])
 
-        for step in STEPS:
-            parts = step.split(":")
-            op = parts[0]
-            eng = parts[1] if len(parts) > 1 else "s"
-            if op == "touch":
-                for i in TOUCH:
-                    src = planes[3][:, 0:4].rearrange("p (t o) -> p t o", o=1)
-                    if eng == "v":
-                        nc.vector.tensor_copy(g4s[i][:, :, 0:1], src)
-                    else:
-                        nc.scalar.copy(g4s[i][:, :, 0:1], src)
-            elif op == "cast":
-                for t in [int(v) for v in parts[2].split(",")]:
-                    if eng == "g":
-                        nc.gpsimd.tensor_scalar(xb[:, t, :], planes[t][:], 1.0, 0.0, MULT, ADD)
-                    else:
-                        nc.scalar.copy(xb[:, t, :], planes[t][:])
-            elif op == "f":
-                experts = [int(v) for v in eng.split(",")]
-                for e in experts:
-                    gf = held.tile([P, C, 4], BF16, name="grouped_f%d" % e, align_bytes=64)
-                    groups["f%d" % e] = (e * C, C, gf)
-                for t in range(4):
-                    for e in experts:
-                        nc.scalar.activation(groups["f%d" % e][2][:, :, t], xb[:, t, :].indirect(offs_t[:, e * (C // 16):(e + 1) * (C // 16)]), COPY)
-            elif op.startswith("mf"):
-                multiply(*groups[op[1:]], eng)
-            elif op.startswith("f"):
-                e = int(op[1:])
-                gf = held.tile([P, C, 4], BF16, name="grouped_f%d" % e, align_bytes=64)
-                for t in range(4):
-                    nc.scalar.activation(gf[:, :, t], xb[:, t, :].indirect(offs_t[:, e * (C // 16):(e + 1) * (C // 16)]), COPY)
-                groups[op] = (e * C, C, gf)
-            elif op.startswith("g"):
-                i = int(op[1:])
-                slot0, n = CUTS[i]
-                g4 = g4s[i]
-                cols = offs_t[:, slot0 // 16:(slot0 + n) // 16]
-                for t in range(4):
-                    nc.vector.tensor_copy(g4[:, t, :], planes[t][:].indirect(cols))
-            elif op.startswith("il"):
-                i = int(op[2:])
-                slot0, n = CUTS[i]
-                gr = held.tile([P, n, 4], BF16, name="grouped%d" % i, align_bytes=64)
-                src = g4s[i][:].rearrange("p t c -> p c t")
-                if eng == "v":
-                    nc.vector.tensor_copy(gr[:], src)
-                elif eng == "g":
-                    nc.gpsimd.tensor_scalar(gr[:], src, 1.0, 0.0, MULT, ADD)
-                else:
-                    nc.scalar.copy(gr[:], src)
-                groups[str(i)] = (slot0, n, gr)
-            elif op.startswith("m"):
-                multiply(*groups[op[1:]], eng)
+        nc.scalar.copy(planes_bf[:, 0, :], planes[0][:])
+        for i in range(1, len(VECTOR_GROUPS)):
+            nc.scalar.copy(gathered[i][:, :, 0:1], planes[PACK - 1][:, 0:PACK].rearrange("p (t o) -> p t o", o=1))
+        for t in range(1, PACK):
+            nc.gpsimd.tensor_scalar(planes_bf[:, t, :], planes[t][:], 1.0, 0.0, MULT, ADD)
 
-        t0 = 0
-        for h, n in enumerate(PIECES):
-            tok = slice(t0, t0 + n)
-            cols = slice(t0 // 16, (t0 + n) // 16)
-            first = held.tile([P, n], F32, name="first%d" % h)
-            second = held.tile([P, n], F32, name="second%d" % h)
-            total = held.tile([P, n], F32, name="total%d" % h)
-            nc.vector.tensor_tensor(first[:], y[:].indirect(pos1_t[:, cols]), gate_t[:, 0, tok], MULT)
-            nc.vector.tensor_tensor(second[:], y[:].indirect(pos2_t[:, cols]), gate_t[:, 1, tok], MULT)
-            nc.vector.tensor_tensor(total[:], first[:], second[:], ADD)
-            nc.sync.dma_start(out[:, tok], total[:])
-            t0 += n
+        gather_on_scalar(*SCALAR_GROUPS[0])
+        for i in range(2):
+            gather_on_vector(i)
+            nc.gpsimd.tensor_scalar(grouped[VECTOR_GROUPS[i][0]][:], interleaved(i), 1.0, 0.0, MULT, ADD)
+        gather_on_scalar(*SCALAR_GROUPS[1])
+        gather_on_vector(2)
+
+        multiply(*SCALAR_GROUPS[0], nc.scalar.copy)
+        multiply(*VECTOR_GROUPS[0], nc.scalar.copy)
+        nc.vector.tensor_copy(grouped[VECTOR_GROUPS[2][0]][:], interleaved(2))
+        multiply(*VECTOR_GROUPS[1], nc.vector.tensor_copy)
+        multiply(*VECTOR_GROUPS[2], nc.scalar.copy)
+        multiply(*SCALAR_GROUPS[1], nc.vector.tensor_copy)
+
+        for t0 in range(0, TOKENS, COMBINE_TOKENS):
+            tokens = slice(t0, t0 + COMBINE_TOKENS)
+            columns = list_columns(t0, COMBINE_TOKENS)
+            first_part = held.tile([P, COMBINE_TOKENS], F32, name="first_part%d" % t0)
+            second_part = held.tile([P, COMBINE_TOKENS], F32, name="second_part%d" % t0)
+            total = held.tile([P, COMBINE_TOKENS], F32, name="total%d" % t0)
+            nc.vector.tensor_tensor(first_part[:], y[:].indirect(pos1_t[:, columns]), gate_t[:, 0, tokens], MULT)
+            nc.vector.tensor_tensor(second_part[:], y[:].indirect(pos2_t[:, columns]), gate_t[:, 1, tokens], MULT)
+            nc.vector.tensor_tensor(total[:], first_part[:], second_part[:], ADD)
+            nc.sync.dma_start(out[:, tokens], total[:])

@@ -125,13 +125,14 @@ def tile_routed_moe_kernel(tc, xT, w_words, w_scales, gate, offs, pos1, pos2, ou
         multiply(*VECTOR_GROUPS[2], nc.scalar.copy)
         multiply(*SCALAR_GROUPS[1], nc.vector.tensor_copy)
 
-        for t0 in range(0, TOKENS, COMBINE_TOKENS):
-            tokens = slice(t0, t0 + COMBINE_TOKENS)
-            columns = list_columns(t0, COMBINE_TOKENS)
-            first_part = held.tile([P, COMBINE_TOKENS], F32, name="first_part%d" % t0)
-            second_part = held.tile([P, COMBINE_TOKENS], F32, name="second_part%d" % t0)
-            total = held.tile([P, COMBINE_TOKENS], F32, name="total%d" % t0)
-            nc.vector.tensor_tensor(first_part[:], y[:].indirect(pos1_t[:, columns]), gate_t[:, 0, tokens], MULT)
-            nc.vector.tensor_tensor(second_part[:], y[:].indirect(pos2_t[:, columns]), gate_t[:, 1, tokens], MULT)
-            nc.vector.tensor_tensor(total[:], first_part[:], second_part[:], ADD)
+        first_part = held.tile([P, TOKENS], F32, name="first_part")
+        second_part = held.tile([P, TOKENS], F32, name="second_part")
+        pieces = [slice(t0, t0 + COMBINE_TOKENS) for t0 in range(0, TOKENS, COMBINE_TOKENS)]
+        nc.vector.tensor_tensor(first_part[:], y[:].indirect(pos1_t[:]), gate_t[:, 0, :], MULT)
+        for tokens in pieces:
+            columns = list_columns(tokens.start, COMBINE_TOKENS)
+            nc.vector.tensor_tensor(second_part[:, tokens], y[:].indirect(pos2_t[:, columns]), gate_t[:, 1, tokens], MULT)
+        for tokens in pieces:
+            total = held.tile([P, COMBINE_TOKENS], F32, name="total%d" % tokens.start)
+            nc.vector.tensor_tensor(total[:], first_part[:, tokens], second_part[:, tokens], ADD)
             nc.sync.dma_start(out[:, tokens], total[:])

@@ -87,7 +87,7 @@ def tile_routed_moe_kernel(tc, xT, w_words, w_scales, gate, offs, pos1, pos2, ou
                         COPY,
                     )
 
-        def multiply(first, count, copy_out):
+        def multiply(first, count):
             codes = operands.tile([P, count], U32, name="codes", align_bytes=64)
             scale = operands.tile([P, count], U8, name="scale", align_bytes=64)
             nc.vector.quantize_mx(out=codes[:].bitcast(FP8X4), scales=scale[:], in_=grouped[first][:].rearrange("p c t -> p (c t)"))
@@ -103,6 +103,9 @@ def tile_routed_moe_kernel(tc, xT, w_words, w_scales, gate, offs, pos1, pos2, ou
                     start=True,
                     stop=True,
                 )
+            return sums
+
+        def bring_out(first, count, sums, copy_out):
             copy_out(y[:, first:first + count], sums[:])
 
         nc.scalar.copy(planes_bf[:, 0, :], planes[0][:])
@@ -118,12 +121,17 @@ def tile_routed_moe_kernel(tc, xT, w_words, w_scales, gate, offs, pos1, pos2, ou
         gather_on_scalar(*SCALAR_GROUPS[1])
         gather_on_vector(2)
 
-        multiply(*SCALAR_GROUPS[0], nc.scalar.copy)
-        multiply(*VECTOR_GROUPS[0], nc.scalar.copy)
+        sums_s0 = multiply(*SCALAR_GROUPS[0])
+        bring_out(*SCALAR_GROUPS[0], sums_s0, nc.scalar.copy)
+        sums_v0 = multiply(*VECTOR_GROUPS[0])
+        bring_out(*VECTOR_GROUPS[0], sums_v0, nc.scalar.copy)
         nc.vector.tensor_copy(grouped[VECTOR_GROUPS[2][0]][:], interleaved(2))
-        multiply(*VECTOR_GROUPS[1], nc.vector.tensor_copy)
-        multiply(*VECTOR_GROUPS[2], nc.scalar.copy)
-        multiply(*SCALAR_GROUPS[1], nc.vector.tensor_copy)
+        sums_v1 = multiply(*VECTOR_GROUPS[1])
+        sums_v2 = multiply(*VECTOR_GROUPS[2])
+        bring_out(*VECTOR_GROUPS[2], sums_v2, nc.scalar.copy)
+        sums_s1 = multiply(*SCALAR_GROUPS[1])
+        bring_out(*VECTOR_GROUPS[1], sums_v1, nc.vector.tensor_copy)
+        bring_out(*SCALAR_GROUPS[1], sums_s1, nc.scalar.copy)
 
         first_part = held.tile([P, TOKENS], F32, name="first_part")
         second_part = held.tile([P, TOKENS], F32, name="second_part")

@@ -22,6 +22,7 @@ FLOPS = 2 * K * FEATURES * SLOTS
 
 VECTOR_GROUPS = ((0, 256), (256, 256), (512, 128))
 SCALAR_GROUPS = ((640, 256), (896, 128))
+SHARED = 64
 COMBINE_TOKENS = 256
 
 
@@ -73,7 +74,8 @@ def tile_routed_moe_kernel(tc, xT, w_words, w_scales, gate, offs, pos1, pos2, ou
         def gather_on_vector(i):
             first, count = VECTOR_GROUPS[i]
             for t in range(PACK):
-                nc.vector.tensor_copy(gathered[i][:, t, :], planes[t][:].indirect(offs_t[:, list_columns(first, count)]))
+                n = count - SHARED if i == 2 else count
+                nc.vector.tensor_copy(gathered[i][:, t, 0:n], planes[t][:].indirect(offs_t[:, list_columns(first, n)]))
 
         def interleaved(i):
             return gathered[i][:].rearrange("p t c -> p c t")
@@ -110,7 +112,7 @@ def tile_routed_moe_kernel(tc, xT, w_words, w_scales, gate, offs, pos1, pos2, ou
 
         nc.scalar.copy(planes_bf[:, 0, :], planes[0][:])
         for i in range(1, len(VECTOR_GROUPS)):
-            nc.scalar.copy(gathered[i][:, :, 0:1], planes[PACK - 1][:, 0:PACK].rearrange("p (t o) -> p t o", o=1))
+            nc.gpsimd.tensor_scalar(gathered[i][:, :, 0:1], planes[PACK - 1][:, 0:PACK].rearrange("p (t o) -> p t o", o=1), 1.0, 0.0, MULT, ADD)
         for t in range(1, PACK):
             nc.gpsimd.tensor_scalar(planes_bf[:, t, :], planes[t][:], 1.0, 0.0, MULT, ADD)
 
@@ -118,14 +120,22 @@ def tile_routed_moe_kernel(tc, xT, w_words, w_scales, gate, offs, pos1, pos2, ou
         for i in range(2):
             gather_on_vector(i)
             nc.gpsimd.tensor_scalar(grouped[VECTOR_GROUPS[i][0]][:], interleaved(i), 1.0, 0.0, MULT, ADD)
+        last_first, last_count = VECTOR_GROUPS[2]
+        own = last_count - SHARED
+        for t in range(PACK):
+            nc.scalar.activation(
+                grouped[last_first][:, own:last_count, t],
+                planes_bf[:, t, :].indirect(offs_t[:, list_columns(last_first + own, SHARED)]),
+                COPY,
+            )
         gather_on_scalar(*SCALAR_GROUPS[1])
         gather_on_vector(2)
 
-        sums_s0 = multiply(*SCALAR_GROUPS[0])
-        bring_out(*SCALAR_GROUPS[0], sums_s0, nc.scalar.copy)
         sums_v0 = multiply(*VECTOR_GROUPS[0])
         bring_out(*VECTOR_GROUPS[0], sums_v0, nc.scalar.copy)
-        nc.vector.tensor_copy(grouped[VECTOR_GROUPS[2][0]][:], interleaved(2))
+        sums_s0 = multiply(*SCALAR_GROUPS[0])
+        bring_out(*SCALAR_GROUPS[0], sums_s0, nc.scalar.copy)
+        nc.vector.tensor_copy(grouped[last_first][:, 0:own, :], gathered[2][:, :, 0:own].rearrange("p t c -> p c t"))
         sums_v1 = multiply(*VECTOR_GROUPS[1])
         sums_v2 = multiply(*VECTOR_GROUPS[2])
         bring_out(*VECTOR_GROUPS[2], sums_v2, nc.scalar.copy)

@@ -20,9 +20,8 @@ SLOTS = EXPERTS * CAPACITY
 PER_COLUMN = 16
 FLOPS = 2 * K * FEATURES * SLOTS
 
-VECTOR_GROUPS = ((0, 256), (256, 256), (512, 128))
-SCALAR_GROUPS = ((640, 256), (896, 128))
-SHARED = 64
+VECTOR_CUTS = ((0, 288), (288, 192), (480, 96))
+SCALAR_BLOCKS = (((640, 128), (768, 128)), ((576, 64),), ((896, 128),))
 COMBINE_TOKENS = 256
 
 
@@ -36,7 +35,7 @@ def tile_routed_moe_kernel(tc, xT, w_words, w_scales, gate, offs, pos1, pos2, ou
         lists = ctx.enter_context(tc.tile_pool(name="lists", bufs=1))
         held = ctx.enter_context(tc.tile_pool(name="held", bufs=1))
         operands = ctx.enter_context(tc.tile_pool(name="operands", bufs=3))
-        psum = ctx.enter_context(tc.psum_pool(name="psum", bufs=len(VECTOR_GROUPS) + len(SCALAR_GROUPS)))
+        psum = ctx.enter_context(tc.psum_pool(name="psum", bufs=5))
 
         offs_t = lists.tile([P, SLOTS // PER_COLUMN], U16, name="offs_t")
         nc.sync.dma_start(offs_t[:], offs)
@@ -66,33 +65,34 @@ def tile_routed_moe_kernel(tc, xT, w_words, w_scales, gate, offs, pos1, pos2, ou
 
         y = held.tile([P, SLOTS], F32, name="y")
         planes_bf = held.tile([P, PACK, TOKENS], BF16, name="planes_bf")
-        gathered = [held.tile([P, PACK, count], F32, name="gathered%d" % first) for first, count in VECTOR_GROUPS]
-        grouped = {}
-        for first, count in VECTOR_GROUPS + SCALAR_GROUPS:
-            grouped[first] = held.tile([P, count, PACK], BF16, name="grouped%d" % first, align_bytes=64)
+        gathered = [held.tile([P, PACK, count], F32, name="gathered%d" % first) for first, count in VECTOR_CUTS]
+        grouped = held.tile([P, SLOTS, PACK], BF16, name="grouped", align_bytes=64)
 
         def gather_on_vector(i):
-            first, count = VECTOR_GROUPS[i]
+            first, count = VECTOR_CUTS[i]
             for t in range(PACK):
-                n = count - SHARED if i == 2 else count
-                nc.vector.tensor_copy(gathered[i][:, t, 0:n], planes[t][:].indirect(offs_t[:, list_columns(first, n)]))
+                nc.vector.tensor_copy(gathered[i][:, t, :], planes[t][:].indirect(offs_t[:, list_columns(first, count)]))
+
+        def interleave_target(i):
+            first, count = VECTOR_CUTS[i]
+            return grouped[:, first:first + count, :]
 
         def interleaved(i):
             return gathered[i][:].rearrange("p t c -> p c t")
 
-        def gather_on_scalar(first, count):
+        def gather_on_scalar(block):
             for t in range(PACK):
-                for c in range(0, count, CAPACITY):
+                for first, count in block:
                     nc.scalar.activation(
-                        grouped[first][:, c:c + CAPACITY, t],
-                        planes_bf[:, t, :].indirect(offs_t[:, list_columns(first + c, CAPACITY)]),
+                        grouped[:, first:first + count, t],
+                        planes_bf[:, t, :].indirect(offs_t[:, list_columns(first, count)]),
                         COPY,
                     )
 
         def multiply(first, count):
             codes = operands.tile([P, count], U32, name="codes", align_bytes=64)
             scale = operands.tile([P, count], U8, name="scale", align_bytes=64)
-            nc.vector.quantize_mx(out=codes[:].bitcast(FP8X4), scales=scale[:], in_=grouped[first][:].rearrange("p c t -> p (c t)"))
+            nc.vector.quantize_mx(out=codes[:].bitcast(FP8X4), scales=scale[:], in_=grouped[:, first:first + count, :].rearrange("p c t -> p (c t)"))
             sums = psum.tile([P, count], F32, name="sums")
             for c in range(0, count, CAPACITY):
                 e = (first + c) // CAPACITY
@@ -111,37 +111,30 @@ def tile_routed_moe_kernel(tc, xT, w_words, w_scales, gate, offs, pos1, pos2, ou
             copy_out(y[:, first:first + count], sums[:])
 
         nc.scalar.copy(planes_bf[:, 0, :], planes[0][:])
-        for i in range(1, len(VECTOR_GROUPS)):
+        for i in range(1, len(VECTOR_CUTS)):
             nc.gpsimd.tensor_scalar(gathered[i][:, :, 0:1], planes[PACK - 1][:, 0:PACK].rearrange("p (t o) -> p t o", o=1), 1.0, 0.0, MULT, ADD)
         for t in range(1, PACK):
             nc.gpsimd.tensor_scalar(planes_bf[:, t, :], planes[t][:], 1.0, 0.0, MULT, ADD)
 
-        gather_on_scalar(*SCALAR_GROUPS[0])
+        gather_on_scalar(SCALAR_BLOCKS[0])
         for i in range(2):
             gather_on_vector(i)
-            nc.gpsimd.tensor_scalar(grouped[VECTOR_GROUPS[i][0]][:], interleaved(i), 1.0, 0.0, MULT, ADD)
-        last_first, last_count = VECTOR_GROUPS[2]
-        own = last_count - SHARED
-        for t in range(PACK):
-            nc.scalar.activation(
-                grouped[last_first][:, own:last_count, t],
-                planes_bf[:, t, :].indirect(offs_t[:, list_columns(last_first + own, SHARED)]),
-                COPY,
-            )
-        gather_on_scalar(*SCALAR_GROUPS[1])
+            nc.gpsimd.tensor_scalar(interleave_target(i), interleaved(i), 1.0, 0.0, MULT, ADD)
+        gather_on_scalar(SCALAR_BLOCKS[1])
+        gather_on_scalar(SCALAR_BLOCKS[2])
         gather_on_vector(2)
 
-        sums_v0 = multiply(*VECTOR_GROUPS[0])
-        bring_out(*VECTOR_GROUPS[0], sums_v0, nc.scalar.copy)
-        sums_s0 = multiply(*SCALAR_GROUPS[0])
-        bring_out(*SCALAR_GROUPS[0], sums_s0, nc.scalar.copy)
-        nc.vector.tensor_copy(grouped[last_first][:, 0:own, :], gathered[2][:, :, 0:own].rearrange("p t c -> p c t"))
-        sums_v1 = multiply(*VECTOR_GROUPS[1])
-        sums_v2 = multiply(*VECTOR_GROUPS[2])
-        bring_out(*VECTOR_GROUPS[2], sums_v2, nc.scalar.copy)
-        sums_s1 = multiply(*SCALAR_GROUPS[1])
-        bring_out(*VECTOR_GROUPS[1], sums_v1, nc.vector.tensor_copy)
-        bring_out(*SCALAR_GROUPS[1], sums_s1, nc.scalar.copy)
+        sums_a = multiply(0, 256)
+        bring_out(0, 256, sums_a, nc.scalar.copy)
+        nc.vector.tensor_copy(interleave_target(2), interleaved(2))
+        sums_b = multiply(640, 256)
+        bring_out(640, 256, sums_b, nc.scalar.copy)
+        sums_c = multiply(256, 256)
+        sums_d = multiply(512, 128)
+        bring_out(512, 128, sums_d, nc.scalar.copy)
+        sums_e = multiply(896, 128)
+        bring_out(256, 256, sums_c, nc.vector.tensor_copy)
+        bring_out(896, 128, sums_e, nc.scalar.copy)
 
         first_part = held.tile([P, TOKENS], F32, name="first_part")
         second_part = held.tile([P, TOKENS], F32, name="second_part")

@@ -20,7 +20,7 @@ SLOTS = EXPERTS * CAPACITY
 PER_COLUMN = 16
 FLOPS = 2 * K * FEATURES * SLOTS
 
-VECTOR_CUTS = ((0, 288), (288, 192), (480, 96))
+VECTOR_CUTS = ((0, 256), (256, 320))
 SCALAR_BLOCKS = (((640, 128), (768, 128)), ((576, 64),), ((896, 128),))
 COMBINE_TOKENS = 256
 
@@ -117,16 +117,15 @@ def tile_routed_moe_kernel(tc, xT, w_words, w_scales, gate, offs, pos1, pos2, ou
             nc.gpsimd.tensor_scalar(planes_bf[:, t, :], planes[t][:], 1.0, 0.0, MULT, ADD)
 
         gather_on_scalar(SCALAR_BLOCKS[0])
-        for i in range(2):
-            gather_on_vector(i)
-            nc.gpsimd.tensor_scalar(interleave_target(i), interleaved(i), 1.0, 0.0, MULT, ADD)
+        gather_on_vector(0)
+        nc.gpsimd.tensor_scalar(interleave_target(0), interleaved(0), 1.0, 0.0, MULT, ADD)
+        gather_on_vector(1)
         gather_on_scalar(SCALAR_BLOCKS[1])
         gather_on_scalar(SCALAR_BLOCKS[2])
-        gather_on_vector(2)
 
         sums_a = multiply(0, 256)
         bring_out(0, 256, sums_a, nc.scalar.copy)
-        nc.vector.tensor_copy(interleave_target(2), interleaved(2))
+        nc.vector.tensor_copy(interleave_target(1), interleaved(1))
         sums_b = multiply(640, 256)
         bring_out(640, 256, sums_b, nc.scalar.copy)
         sums_c = multiply(256, 256)

@@ -125,7 +125,10 @@ def tile_routed_moe_kernel(tc, xT, w_words, w_scales, gate, offs, pos1, pos2, ou
 
         sums_a = multiply(0, 256)
         bring_out(0, 256, sums_a, nc.scalar.copy)
-        nc.vector.tensor_copy(interleave_target(1), interleaved(1))
+        nc.vector.tensor_copy(
+            interleave_target(1).rearrange("p (c i) t -> p c t i", i=4),
+            gathered[1][:].rearrange("p t (c i) -> p c t i", i=4),
+        )
         sums_b = multiply(640, 256)
         bring_out(640, 256, sums_b, nc.scalar.copy)
         sums_c = multiply(256, 256)

@@ -20,9 +20,9 @@ SLOTS = EXPERTS * CAPACITY
 PER_COLUMN = 16
 FLOPS = 2 * K * FEATURES * SLOTS
 
-VECTOR_CUTS = ((0, 256), (256, 320))
+VECTOR_CUTS = ((0, 288), (288, 288))
 SCALAR_BLOCKS = (((640, 128), (768, 128)), ((576, 64),), ((896, 128),))
-COMBINE_TOKENS = 256
+COMBINE_TOKENS = 320
 
 
 def list_columns(first, count):
@@ -38,14 +38,14 @@ def tile_routed_moe_kernel(tc, xT, w_words, w_scales, gate, offs, pos1, pos2, ou
         psum = ctx.enter_context(tc.psum_pool(name="psum", bufs=5))
 
         offs_t = lists.tile([P, SLOTS // PER_COLUMN], U16, name="offs_t")
-        nc.sync.dma_start(offs_t[:], offs)
-
         planes = []
         x_planes = xT.rearrange("(p t) n -> t p n", t=PACK)
         for t in range(PACK):
             plane = held.tile([P, TOKENS], F32, name="plane%d" % t)
             nc.sync.dma_start(plane[:], x_planes[t])
             planes.append(plane)
+            if t == 0:
+                nc.sync.dma_start(offs_t[:], offs)
 
         w_codes = held.tile([P, EXPERTS, FEATURES], U32, name="w_codes", align_bytes=64)
         nc.sync.dma_start(w_codes[:].bitcast(I32), w_words.rearrange("e a p n r -> p (e a) (n r)").bitcast(I32))
@@ -140,12 +140,12 @@ def tile_routed_moe_kernel(tc, xT, w_words, w_scales, gate, offs, pos1, pos2, ou
 
         first_part = held.tile([P, TOKENS], F32, name="first_part")
         second_part = held.tile([P, TOKENS], F32, name="second_part")
-        pieces = [slice(t0, t0 + COMBINE_TOKENS) for t0 in range(0, TOKENS, COMBINE_TOKENS)]
+        pieces = [slice(0, COMBINE_TOKENS), slice(COMBINE_TOKENS, TOKENS)]
         nc.vector.tensor_tensor(first_part[:], y[:].indirect(pos1_t[:]), gate_t[:, 0, :], MULT)
         for tokens in pieces:
-            columns = list_columns(tokens.start, COMBINE_TOKENS)
+            columns = list_columns(tokens.start, tokens.stop - tokens.start)
             nc.vector.tensor_tensor(second_part[:, tokens], y[:].indirect(pos2_t[:, columns]), gate_t[:, 1, tokens], MULT)
         for tokens in pieces:
-            total = held.tile([P, COMBINE_TOKENS], F32, name="total%d" % tokens.start)
+            total = held.tile([P, tokens.stop - tokens.start], F32, name="total%d" % tokens.start)
             nc.vector.tensor_tensor(total[:], first_part[:, tokens], second_part[:, tokens], ADD)
             nc.sync.dma_start(out[:, tokens], total[:])

@@ -20,8 +20,8 @@ SLOTS = EXPERTS * CAPACITY
 PER_COLUMN = 16
 FLOPS = 2 * K * FEATURES * SLOTS
 
-VECTOR_CUTS = ((0, 288), (288, 288))
-SCALAR_BLOCKS = (((640, 128), (768, 128)), ((576, 64),), ((896, 128),))
+VECTOR_CUTS = ((0, 256), (256, 256))
+SCALAR_BLOCKS = (((512, 128), (640, 128)), ((768, 128),), ((896, 128),))
 COMBINE_TOKENS = 320
 
 
@@ -129,11 +129,11 @@ def tile_routed_moe_kernel(tc, xT, w_words, w_scales, gate, offs, pos1, pos2, ou
             interleave_target(1).rearrange("p (c i) t -> p c t i", i=4),
             gathered[1][:].rearrange("p t (c i) -> p c t i", i=4),
         )
-        sums_b = multiply(640, 256)
-        bring_out(640, 256, sums_b, nc.scalar.copy)
         sums_c = multiply(256, 256)
-        sums_d = multiply(512, 128)
-        bring_out(512, 128, sums_d, nc.scalar.copy)
+        sums_b = multiply(512, 256)
+        bring_out(512, 256, sums_b, nc.scalar.copy)
+        sums_d = multiply(768, 128)
+        bring_out(768, 128, sums_d, nc.scalar.copy)
         sums_e = multiply(896, 128)
         bring_out(256, 256, sums_c, nc.vector.tensor_copy)
         bring_out(896, 128, sums_e, nc.scalar.copy)

@@ -22,6 +22,7 @@ FLOPS = 2 * K * FEATURES * SLOTS
 
 VECTOR_CUTS = ((0, 256), (256, 256))
 SCALAR_BLOCKS = (((512, 128), (640, 128)), ((768, 128),), ((896, 128),))
+HALVES = (slice(0, TOKENS // 2), slice(TOKENS // 2, TOKENS))
 COMBINE_TOKENS = 320
 
 
@@ -37,15 +38,22 @@ def tile_routed_moe_kernel(tc, xT, w_words, w_scales, gate, offs, pos1, pos2, ou
         operands = ctx.enter_context(tc.tile_pool(name="operands", bufs=3))
         psum = ctx.enter_context(tc.psum_pool(name="psum", bufs=5))
 
+        warm = held.tile([P, 2], F32, name="warm")
+        nc.vector.memset(warm[:, 0:1], 0.0)
+        nc.scalar.activation(warm[:, 1:2], warm[:, 0:1], COPY)
+
         offs_t = lists.tile([P, SLOTS // PER_COLUMN], U16, name="offs_t")
         planes = []
         x_planes = xT.rearrange("(p t) n -> t p n", t=PACK)
         for t in range(PACK):
             plane = held.tile([P, TOKENS], F32, name="plane%d" % t)
-            nc.sync.dma_start(plane[:], x_planes[t])
             planes.append(plane)
             if t == 0:
+                for tokens in HALVES:
+                    nc.sync.dma_start(plane[:, tokens], x_planes[t][:, tokens])
                 nc.sync.dma_start(offs_t[:], offs)
+            else:
+                nc.sync.dma_start(plane[:], x_planes[t])
 
         w_codes = held.tile([P, EXPERTS, FEATURES], U32, name="w_codes", align_bytes=64)
         nc.sync.dma_start(w_codes[:].bitcast(I32), w_words.rearrange("e a p n r -> p (e a) (n r)").bitcast(I32))
@@ -110,7 +118,8 @@ def tile_routed_moe_kernel(tc, xT, w_words, w_scales, gate, offs, pos1, pos2, ou
         def bring_out(first, count, sums, copy_out):
             copy_out(y[:, first:first + count], sums[:])
 
-        nc.scalar.copy(planes_bf[:, 0, :], planes[0][:])
+        for tokens in HALVES:
+            nc.vector.tensor_copy(planes_bf[:, 0, tokens], planes[0][:, tokens])
         for i in range(1, len(VECTOR_CUTS)):
             nc.gpsimd.tensor_scalar(gathered[i][:, :, 0:1], planes[PACK - 1][:, 0:PACK].rearrange("p (t o) -> p t o", o=1), 1.0, 0.0, MULT, ADD)
         for t in range(1, PACK):

@@ -20,7 +20,7 @@ SLOTS = EXPERTS * CAPACITY
 PER_COLUMN = 16
 FLOPS = 2 * K * FEATURES * SLOTS
 
-VECTOR_CUTS = ((0, 256), (256, 256))
+VECTOR_CUTS = ((0, 320), (320, 192))
 SCALAR_BLOCKS = (((512, 128), (640, 128)), ((768, 128),), ((896, 128),))
 HALVES = (slice(0, TOKENS // 2), slice(TOKENS // 2, TOKENS))
 COMBINE_TOKENS = 320
@@ -121,7 +121,7 @@ def tile_routed_moe_kernel(tc, xT, w_words, w_scales, gate, offs, pos1, pos2, ou
         for tokens in HALVES:
             nc.vector.tensor_copy(planes_bf[:, 0, tokens], planes[0][:, tokens])
         for i in range(1, len(VECTOR_CUTS)):
-            nc.gpsimd.tensor_scalar(gathered[i][:, :, 0:1], planes[PACK - 1][:, 0:PACK].rearrange("p (t o) -> p t o", o=1), 1.0, 0.0, MULT, ADD)
+            nc.gpsimd.tensor_scalar(gathered[i][:, :, 0:1], planes[PACK - 2][:, 0:PACK].rearrange("p (t o) -> p t o", o=1), 1.0, 0.0, MULT, ADD)
         for t in range(1, PACK):
             nc.gpsimd.tensor_scalar(planes_bf[:, t, :], planes[t][:], 1.0, 0.0, MULT, ADD)
 

from contextlib import ExitStack

import concourse.mybir as mybir

F32 = mybir.dt.float32
BF16 = mybir.dt.bfloat16
U32 = mybir.dt.uint32
I32 = mybir.dt.int32
U16 = mybir.dt.uint16
U8 = mybir.dt.uint8
FP8X4 = mybir.dt.float8_e4m3fn_x4
MULT = mybir.AluOpType.mult
ADD = mybir.AluOpType.add
COPY = mybir.ActivationFunctionType.Copy

P = 128
PACK = 4
K, TOKENS, EXPERTS, CAPACITY, FEATURES = 512, 512, 8, 128, 128
SLOTS = EXPERTS * CAPACITY
PER_COLUMN = 16
FLOPS = 2 * K * FEATURES * SLOTS

VECTOR_CUTS = ((0, 320), (320, 192))
SCALAR_BLOCKS = (((512, 128), (640, 128)), ((768, 128),), ((896, 128),))
HALVES = (slice(0, TOKENS // 2), slice(TOKENS // 2, TOKENS))
COMBINE_TOKENS = 320


def list_columns(first, count):
    return slice(first // PER_COLUMN, (first + count) // PER_COLUMN)


def tile_routed_moe_kernel(tc, xT, w_words, w_scales, gate, offs, pos1, pos2, out):
    nc = tc.nc
    with ExitStack() as ctx:
        lists = ctx.enter_context(tc.tile_pool(name="lists", bufs=1))
        held = ctx.enter_context(tc.tile_pool(name="held", bufs=1))
        operands = ctx.enter_context(tc.tile_pool(name="operands", bufs=3))
        psum = ctx.enter_context(tc.psum_pool(name="psum", bufs=5))

        warm = held.tile([P, 2], F32, name="warm")
        nc.vector.memset(warm[:, 0:1], 0.0)
        nc.scalar.activation(warm[:, 1:2], warm[:, 0:1], COPY)

        offs_t = lists.tile([P, SLOTS // PER_COLUMN], U16, name="offs_t")
        planes = []
        x_planes = xT.rearrange("(p t) n -> t p n", t=PACK)
        for t in range(PACK):
            plane = held.tile([P, TOKENS], F32, name="plane%d" % t)
            planes.append(plane)
            if t == 0:
                for tokens in HALVES:
                    nc.sync.dma_start(plane[:, tokens], x_planes[t][:, tokens])
                nc.sync.dma_start(offs_t[:], offs)
            else:
                nc.sync.dma_start(plane[:], x_planes[t])

        w_codes = held.tile([P, EXPERTS, FEATURES], U32, name="w_codes", align_bytes=64)
        nc.sync.dma_start(w_codes[:].bitcast(I32), w_words.rearrange("e a p n r -> p (e a) (n r)").bitcast(I32))

        w_scale = held.tile([P, EXPERTS, FEATURES], U8, name="w_scale", align_bytes=64)
        nc.vector.memset(w_scale[:].rearrange("p e n -> p (e n)").bitcast(I32), 0)
        scale_rows = w_scales.rearrange("e a (q r) n -> r q (e a) n", r=4)
        for r in range(4):
            nc.sync.dma_start(w_scale[r:P:32, :, :].bitcast(I32), scale_rows[r].bitcast(I32))

        pos1_t = lists.tile([P, TOKENS // PER_COLUMN], U16, name="pos1_t")
        nc.sync.dma_start(pos1_t[:], pos1)
        pos2_t = lists.tile([P, TOKENS // PER_COLUMN], U16, name="pos2_t")
        nc.sync.dma_start(pos2_t[:], pos2)
        gate_t = held.tile([P, 2, TOKENS], F32, name="gate_t")
        nc.sync.dma_start(gate_t[:], gate.rearrange("g n t -> n g t"))

        y = held.tile([P, SLOTS], F32, name="y")
        planes_bf = held.tile([P, PACK, TOKENS], BF16, name="planes_bf")
        gathered = [held.tile([P, PACK, count], F32, name="gathered%d" % first) for first, count in VECTOR_CUTS]
        grouped = held.tile([P, SLOTS, PACK], BF16, name="grouped", align_bytes=64)

        def gather_on_vector(i):
            first, count = VECTOR_CUTS[i]
            for t in range(PACK):
                nc.vector.tensor_copy(gathered[i][:, t, :], planes[t][:].indirect(offs_t[:, list_columns(first, count)]))

        def interleave_target(i):
            first, count = VECTOR_CUTS[i]
            return grouped[:, first:first + count, :]

        def interleaved(i):
            return gathered[i][:].rearrange("p t c -> p c t")

        def gather_on_scalar(block):
            for t in range(PACK):
                for first, count in block:
                    nc.scalar.activation(
                        grouped[:, first:first + count, t],
                        planes_bf[:, t, :].indirect(offs_t[:, list_columns(first, count)]),
                        COPY,
                    )

        def multiply(first, count):
            codes = operands.tile([P, count], U32, name="codes", align_bytes=64)
            scale = operands.tile([P, count], U8, name="scale", align_bytes=64)
            nc.vector.quantize_mx(out=codes[:].bitcast(FP8X4), scales=scale[:], in_=grouped[:, first:first + count, :].rearrange("p c t -> p (c t)"))
            sums = psum.tile([P, count], F32, name="sums")
            for c in range(0, count, CAPACITY):
                e = (first + c) // CAPACITY
                nc.tensor.matmul_mx(
                    out=sums[:, c:c + CAPACITY],
                    lhsT=w_codes[:, e, :].bitcast(FP8X4),
                    lhsT_scale=w_scale[:, e, :],
                    rhs=codes[:, c:c + CAPACITY].bitcast(FP8X4),
                    rhs_scale=scale[:, c:c + CAPACITY],
                    start=True,
                    stop=True,
                )
            return sums

        def bring_out(first, count, sums, copy_out):
            copy_out(y[:, first:first + count], sums[:])

        for tokens in HALVES:
            nc.vector.tensor_copy(planes_bf[:, 0, tokens], planes[0][:, tokens])
        for i in range(1, len(VECTOR_CUTS)):
            nc.gpsimd.tensor_scalar(gathered[i][:, :, 0:1], planes[PACK - 2][:, 0:PACK].rearrange("p (t o) -> p t o", o=1), 1.0, 0.0, MULT, ADD)
        for t in range(1, PACK):
            nc.gpsimd.tensor_scalar(planes_bf[:, t, :], planes[t][:], 1.0, 0.0, MULT, ADD)

        gather_on_scalar(SCALAR_BLOCKS[0])
        gather_on_vector(0)
        nc.gpsimd.tensor_scalar(interleave_target(0), interleaved(0), 1.0, 0.0, MULT, ADD)
        gather_on_vector(1)
        gather_on_scalar(SCALAR_BLOCKS[1])
        gather_on_scalar(SCALAR_BLOCKS[2])

        sums_a = multiply(0, 256)
        bring_out(0, 256, sums_a, nc.scalar.copy)
        nc.vector.tensor_copy(
            interleave_target(1).rearrange("p (c i) t -> p c t i", i=4),
            gathered[1][:].rearrange("p t (c i) -> p c t i", i=4),
        )
        sums_c = multiply(256, 256)
        sums_b = multiply(512, 256)
        bring_out(512, 256, sums_b, nc.scalar.copy)
        sums_d = multiply(768, 128)
        bring_out(768, 128, sums_d, nc.scalar.copy)
        sums_e = multiply(896, 128)
        bring_out(256, 256, sums_c, nc.vector.tensor_copy)
        bring_out(896, 128, sums_e, nc.scalar.copy)

        first_part = held.tile([P, TOKENS], F32, name="first_part")
        second_part = held.tile([P, TOKENS], F32, name="second_part")
        pieces = [slice(0, COMBINE_TOKENS), slice(COMBINE_TOKENS, TOKENS)]
        nc.vector.tensor_tensor(first_part[:], y[:].indirect(pos1_t[:]), gate_t[:, 0, :], MULT)
        for tokens in pieces:
            columns = list_columns(tokens.start, tokens.stop - tokens.start)
            nc.vector.tensor_tensor(second_part[:, tokens], y[:].indirect(pos2_t[:, columns]), gate_t[:, 1, tokens], MULT)
        for tokens in pieces:
            total = held.tile([P, tokens.stop - tokens.start], F32, name="total%d" % tokens.start)
            nc.vector.tensor_tensor(total[:], first_part[:, tokens], second_part[:, tokens], ADD)
            nc.sync.dma_start(out[:, tokens], total[:])
